import numpy as np
import ml_dtypes

BF16 = ml_dtypes.bfloat16


def bf(x):
    return np.asarray(x, np.float32).astype(BF16)


def f32(x):
    return np.asarray(x, np.float32)


def f64(x):
    return np.asarray(x).astype(np.float64)


def striped(idx):
    return np.tile(idx.reshape(-1, 16).T, (8, 1))


S, K, M, N, D, V = 1024, 256, 128, 768, 8, 96


def gelu_tanh(v):
    return 0.5 * v * (1.0 + np.tanh(np.sqrt(2.0 / np.pi) * (v + 0.044715 * v**3)))


def setup_inputs():
    return {"table": bf(np.random.standard_normal((K, S))), "w": bf(np.random.standard_normal((K, M)) / np.sqrt(K)), "b": f32(0.5 * np.random.standard_normal((M, 1))), "offs": striped(np.random.permutation(np.tile(np.arange(S), 2))[:N])}


def reference(table, w, b, offs):
    idx = offs[:16].T.reshape(-1)
    x = f64(table)[:, idx]
    y = f64(w).T @ x
    z = gelu_tanh(y + f64(b))
    return z.reshape(M, V, D).mean(axis=2)

@@ -1,0 +1,55 @@
+import concourse.mybir as mybir
+
+BF16, F32, U16 = mybir.dt.bfloat16, mybir.dt.float32, mybir.dt.uint16
+GELU_TANH = mybir.ActivationFunctionType.Gelu_apprx_tanh
+
+P = 128
+S = 1024
+K_BLOCKS = 2
+N = 768
+PIECE = 384
+PIECES = N // PIECE
+GROUP = 8
+POOLED = PIECE // GROUP
+
+FLOPS = 2 * K_BLOCKS * P * P * N
+
+
+def tile_gather_matmul_kernel(tc, table, w, b, offs, out):
+    nc = tc.nc
+    with (
+        tc.tile_pool(name="held", bufs=1) as held,
+        tc.tile_pool(name="work", bufs=2) as work,
+        tc.psum_pool(name="psum", bufs=2) as psum,
+    ):
+        offsets = held.tile([P, N // 16], U16, name="offsets")
+        nc.sync.dma_start(offsets[:], offs)
+
+        weights = held.tile([P, K_BLOCKS, P], BF16, name="weights")
+        nc.scalar.dma_start(weights[:], w.rearrange("(a p) m -> p a m", p=P))
+
+        blocks = [held.tile([P, S], BF16, name="block%d" % a) for a in range(K_BLOCKS)]
+        nc.sync.dma_start(blocks[0][:], table[0:P, :])
+        nc.scalar.dma_start(blocks[1][:], table[P : 2 * P, :])
+
+        bias = held.tile([P, 1], F32, name="bias")
+        nc.gpsimd.dma_start(bias[:], b)
+
+        means = held.tile([P, N // GROUP], F32, name="means")
+        for piece in range(PIECES):
+            picked = offsets[:, piece * (PIECE // 16) : (piece + 1) * (PIECE // 16)]
+            y = psum.tile([P, PIECE], F32, name="y")
+            for a in range(K_BLOCKS):
+                nc.tensor.matmul(
+                    y[:],
+                    weights[:, a, :],
+                    blocks[a][:].indirect(picked),
+                    start=(a == 0),
+                    stop=(a == K_BLOCKS - 1),
+                )
+            z = work.tile([P, PIECE], F32, name="z")
+            nc.scalar.activation(z[:], y[:], GELU_TANH, bias=bias[:, 0:1])
+            sums = work.tile([P, POOLED], F32, name="sums")
+            nc.vector.reduce_sum(sums[:], z[:].rearrange("p (v t) -> p v t", t=GROUP), axis=mybir.AxisListType.X)
+            nc.vector.tensor_scalar_mul(means[:, piece * POOLED : (piece + 1) * POOLED], sums[:], 1.0 / GROUP)
+        nc.sync.dma_start(out, means[:])

@@ -7,10 +7,12 @@ P = 128
 S = 1024
 K_BLOCKS = 2
 N = 768
-PIECE = 384
+PIECE = 256
 PIECES = N // PIECE
 GROUP = 8
 POOLED = PIECE // GROUP
+BANK = 512
+WARM_UPS = 4
 
 FLOPS = 2 * K_BLOCKS * P * P * N
 
@@ -20,36 +22,45 @@ def tile_gather_matmul_kernel(tc, table, w, b, offs, out):
     with (
         tc.tile_pool(name="held", bufs=1) as held,
         tc.tile_pool(name="work", bufs=2) as work,
-        tc.psum_pool(name="psum", bufs=2) as psum,
+        tc.psum_pool(name="psum", bufs=1) as psum,
     ):
         offsets = held.tile([P, N // 16], U16, name="offsets")
         nc.sync.dma_start(offsets[:], offs)
+        blocks = [held.tile([P, S], BF16, name="block%d" % a) for a in range(K_BLOCKS)]
+        for a in range(K_BLOCKS):
+            nc.sync.dma_start(blocks[a][:], table[a * P : (a + 1) * P, :])
 
         weights = held.tile([P, K_BLOCKS, P], BF16, name="weights")
         nc.scalar.dma_start(weights[:], w.rearrange("(a p) m -> p a m", p=P))
-
-        blocks = [held.tile([P, S], BF16, name="block%d" % a) for a in range(K_BLOCKS)]
-        nc.sync.dma_start(blocks[0][:], table[0:P, :])
-        nc.scalar.dma_start(blocks[1][:], table[P : 2 * P, :])
-
         bias = held.tile([P, 1], F32, name="bias")
-        nc.gpsimd.dma_start(bias[:], b)
+        nc.scalar.dma_start(bias[:], b)
 
-        means = held.tile([P, N // GROUP], F32, name="means")
-        for piece in range(PIECES):
-            picked = offsets[:, piece * (PIECE // 16) : (piece + 1) * (PIECE // 16)]
-            y = psum.tile([P, PIECE], F32, name="y")
-            for a in range(K_BLOCKS):
+        zeros = held.tile([P, BANK], BF16, name="zeros")
+        nc.gpsimd.memset(zeros[:], 0.0)
+        warmed = held.tile([P, 1], F32, name="warmed")
+        nc.scalar.activation(warmed[:], zeros[:, 0:1], GELU_TANH)
+
+        idle = psum.tile([P, BANK], F32, name="idle")
+        for i in range(WARM_UPS):
+            nc.tensor.matmul(idle[:], zeros[:, 0:P], zeros[:], start=True, stop=True)
+
+        y = [psum.tile([P, PIECE], F32, name="y%d" % piece) for piece in range(PIECES)]
+        for a in range(K_BLOCKS):
+            for piece in range(PIECES):
+                picked = offsets[:, piece * (PIECE // 16) : (piece + 1) * (PIECE // 16)]
                 nc.tensor.matmul(
-                    y[:],
+                    y[piece][:],
                     weights[:, a, :],
                     blocks[a][:].indirect(picked),
                     start=(a == 0),
                     stop=(a == K_BLOCKS - 1),
                 )
+
+        means = held.tile([P, N // GROUP], F32, name="means")
+        for piece in range(PIECES):
             z = work.tile([P, PIECE], F32, name="z")
-            nc.scalar.activation(z[:], y[:], GELU_TANH, bias=bias[:, 0:1])
-            sums = work.tile([P, POOLED], F32, name="sums")
-            nc.vector.reduce_sum(sums[:], z[:].rearrange("p (v t) -> p v t", t=GROUP), axis=mybir.AxisListType.X)
-            nc.vector.tensor_scalar_mul(means[:, piece * POOLED : (piece + 1) * POOLED], sums[:], 1.0 / GROUP)
+            nc.scalar.activation(z[:], y[piece][:], GELU_TANH, bias=bias[:, 0:1])
+            pooled = work.tile([P, POOLED], F32, name="pooled")
+            nc.vector.reduce_sum(pooled[:], z[:].rearrange("p (v t) -> p v t", t=GROUP), axis=mybir.AxisListType.X)
+            nc.vector.tensor_scalar_mul(means[:, piece * POOLED : (piece + 1) * POOLED], pooled[:], 1.0 / GROUP)
         nc.sync.dma_start(out, means[:])

@@ -11,8 +11,6 @@ PIECE = 256
 PIECES = N // PIECE
 GROUP = 8
 POOLED = PIECE // GROUP
-BANK = 512
-WARM_UPS = 4
 
 FLOPS = 2 * K_BLOCKS * P * P * N
 
@@ -35,14 +33,10 @@ def tile_gather_matmul_kernel(tc, table, w, b, offs, out):
         bias = held.tile([P, 1], F32, name="bias")
         nc.scalar.dma_start(bias[:], b)
 
-        zeros = held.tile([P, BANK], BF16, name="zeros")
+        zeros = held.tile([P, 1], F32, name="zeros")
         nc.gpsimd.memset(zeros[:], 0.0)
         warmed = held.tile([P, 1], F32, name="warmed")
-        nc.scalar.activation(warmed[:], zeros[:, 0:1], GELU_TANH)
-
-        idle = psum.tile([P, BANK], F32, name="idle")
-        for i in range(WARM_UPS):
-            nc.tensor.matmul(idle[:], zeros[:, 0:P], zeros[:], start=True, stop=True)
+        nc.scalar.activation(warmed[:], zeros[:], GELU_TANH)
 
         y = [psum.tile([P, PIECE], F32, name="y%d" % piece) for piece in range(PIECES)]
         for a in range(K_BLOCKS):

@@ -7,10 +7,10 @@ P = 128
 S = 1024
 K_BLOCKS = 2
 N = 768
-PIECE = 256
-PIECES = N // PIECE
 GROUP = 8
-POOLED = PIECE // GROUP
+PIECES = (128, 256, 256, 128)
+STARTS = tuple(sum(PIECES[:piece]) for piece in range(len(PIECES)))
+assert sum(PIECES) == N
 
 FLOPS = 2 * K_BLOCKS * P * P * N
 
@@ -38,10 +38,11 @@ def tile_gather_matmul_kernel(tc, table, w, b, offs, out):
         warmed = held.tile([P, 1], F32, name="warmed")
         nc.scalar.activation(warmed[:], zeros[:], GELU_TANH)
 
-        y = [psum.tile([P, PIECE], F32, name="y%d" % piece) for piece in range(PIECES)]
+        y = [psum.tile([P, PIECES[piece]], F32, name="y%d" % piece) for piece in range(len(PIECES))]
         for a in range(K_BLOCKS):
-            for piece in range(PIECES):
-                picked = offsets[:, piece * (PIECE // 16) : (piece + 1) * (PIECE // 16)]
+            for piece in range(len(PIECES)):
+                first = STARTS[piece] // 16
+                picked = offsets[:, first : first + PIECES[piece] // 16]
                 nc.tensor.matmul(
                     y[piece][:],
                     weights[:, a, :],
@@ -51,10 +52,11 @@ def tile_gather_matmul_kernel(tc, table, w, b, offs, out):
                 )
 
         means = held.tile([P, N // GROUP], F32, name="means")
-        for piece in range(PIECES):
-            z = work.tile([P, PIECE], F32, name="z")
+        for piece in range(len(PIECES)):
+            z = work.tile([P, PIECES[piece]], F32, name="z")
             nc.scalar.activation(z[:], y[piece][:], GELU_TANH, bias=bias[:, 0:1])
-            pooled = work.tile([P, POOLED], F32, name="pooled")
+            pooled = work.tile([P, PIECES[piece] // GROUP], F32, name="pooled")
             nc.vector.reduce_sum(pooled[:], z[:].rearrange("p (v t) -> p v t", t=GROUP), axis=mybir.AxisListType.X)
-            nc.vector.tensor_scalar_mul(means[:, piece * POOLED : (piece + 1) * POOLED], pooled[:], 1.0 / GROUP)
+            first = STARTS[piece] // GROUP
+            nc.vector.tensor_scalar_mul(means[:, first : first + PIECES[piece] // GROUP], pooled[:], 1.0 / GROUP)
         nc.sync.dma_start(out, means[:])

@@ -38,25 +38,38 @@ def tile_gather_matmul_kernel(tc, table, w, b, offs, out):
         warmed = held.tile([P, 1], F32, name="warmed")
         nc.scalar.activation(warmed[:], zeros[:], GELU_TANH)
 
-        y = [psum.tile([P, PIECES[piece]], F32, name="y%d" % piece) for piece in range(len(PIECES))]
-        for a in range(K_BLOCKS):
-            for piece in range(len(PIECES)):
-                first = STARTS[piece] // 16
-                picked = offsets[:, first : first + PIECES[piece] // 16]
-                nc.tensor.matmul(
-                    y[piece][:],
-                    weights[:, a, :],
-                    blocks[a][:].indirect(picked),
-                    start=(a == 0),
-                    stop=(a == K_BLOCKS - 1),
-                )
-
         means = held.tile([P, N // GROUP], F32, name="means")
-        for piece in range(len(PIECES)):
+
+        def look_up(piece, bank, a):
+            first = STARTS[piece] // 16
+            picked = offsets[:, first : first + PIECES[piece] // 16]
+            nc.tensor.matmul(
+                bank[:],
+                weights[:, a, :],
+                blocks[a][:].indirect(picked),
+                start=(a == 0),
+                stop=(a == K_BLOCKS - 1),
+            )
+
+        def finish(piece, bank):
             z = work.tile([P, PIECES[piece]], F32, name="z")
-            nc.scalar.activation(z[:], y[piece][:], GELU_TANH, bias=bias[:, 0:1])
+            nc.scalar.activation(z[:], bank[:], GELU_TANH, bias=bias[:, 0:1])
             pooled = work.tile([P, PIECES[piece] // GROUP], F32, name="pooled")
             nc.vector.reduce_sum(pooled[:], z[:].rearrange("p (v t) -> p v t", t=GROUP), axis=mybir.AxisListType.X)
             first = STARTS[piece] // GROUP
             nc.vector.tensor_scalar_mul(means[:, first : first + PIECES[piece] // GROUP], pooled[:], 1.0 / GROUP)
+
+        last = len(PIECES) - 1
+        banks = [psum.tile([P, PIECES[piece]], F32, name="bank%d" % piece) for piece in range(last)]
+        for a in range(K_BLOCKS):
+            for piece in range(last):
+                look_up(piece, banks[piece], a)
+        finish(0, banks[0])
+
+        bank_again = psum.tile([P, PIECES[last]], F32, name="bank_again", tag="bank0")
+        for a in range(K_BLOCKS):
+            look_up(last, bank_again, a)
+        for piece in range(1, last):
+            finish(piece, banks[piece])
+        finish(last, bank_again)
         nc.sync.dma_start(out, means[:])

@@ -19,7 +19,7 @@ def tile_gather_matmul_kernel(tc, table, w, b, offs, out):
     nc = tc.nc
     with (
         tc.tile_pool(name="held", bufs=1) as held,
-        tc.tile_pool(name="work", bufs=2) as work,
+        tc.tile_pool(name="work", bufs=len(PIECES)) as work,
         tc.psum_pool(name="psum", bufs=1) as psum,
     ):
         offsets = held.tile([P, N // 16], U16, name="offsets")

@@ -40,15 +40,15 @@ def tile_gather_matmul_kernel(tc, table, w, b, offs, out):
 
         means = held.tile([P, N // GROUP], F32, name="means")
 
-        def look_up(piece, bank, a):
+        def look_up(piece, bank, a, opens, closes):
             first = STARTS[piece] // 16
             picked = offsets[:, first : first + PIECES[piece] // 16]
             nc.tensor.matmul(
                 bank[:],
                 weights[:, a, :],
                 blocks[a][:].indirect(picked),
-                start=(a == 0),
-                stop=(a == K_BLOCKS - 1),
+                start=opens,
+                stop=closes,
             )
 
         def finish(piece, bank):
@@ -60,16 +60,12 @@ def tile_gather_matmul_kernel(tc, table, w, b, offs, out):
             nc.vector.tensor_scalar_mul(means[:, first : first + PIECES[piece] // GROUP], pooled[:], 1.0 / GROUP)
 
         last = len(PIECES) - 1
-        banks = [psum.tile([P, PIECES[piece]], F32, name="bank%d" % piece) for piece in range(last)]
+        banks = [psum.tile([P, PIECES[piece]], F32, name="bank%d" % piece) for piece in range(len(PIECES))]
         for a in range(K_BLOCKS):
             for piece in range(last):
-                look_up(piece, banks[piece], a)
-        finish(0, banks[0])
-
-        bank_again = psum.tile([P, PIECES[last]], F32, name="bank_again", tag="bank0")
-        for a in range(K_BLOCKS):
-            look_up(last, bank_again, a)
-        for piece in range(1, last):
+                look_up(piece, banks[piece], a, opens=(a == 0), closes=(a == K_BLOCKS - 1))
+        look_up(last, banks[last], 1, opens=True, closes=False)
+        look_up(last, banks[last], 0, opens=False, closes=True)
+        for piece in range(len(PIECES)):
             finish(piece, banks[piece])
-        finish(last, bank_again)
         nc.sync.dma_start(out, means[:])

@@ -8,7 +8,8 @@ S = 1024
 K_BLOCKS = 2
 N = 768
 GROUP = 8
-PIECES = (128, 256, 256, 128)
+PIECES = (256, 256, 128, 128)
+EARLY = 2
 STARTS = tuple(sum(PIECES[:piece]) for piece in range(len(PIECES)))
 assert sum(PIECES) == N
 
@@ -59,13 +60,13 @@ def tile_gather_matmul_kernel(tc, table, w, b, offs, out):
             first = STARTS[piece] // GROUP
             nc.vector.tensor_scalar_mul(means[:, first : first + PIECES[piece] // GROUP], pooled[:], 1.0 / GROUP)
 
-        last = len(PIECES) - 1
         banks = [psum.tile([P, PIECES[piece]], F32, name="bank%d" % piece) for piece in range(len(PIECES))]
         for a in range(K_BLOCKS):
-            for piece in range(last):
+            for piece in range(EARLY):
                 look_up(piece, banks[piece], a, opens=(a == 0), closes=(a == K_BLOCKS - 1))
-        look_up(last, banks[last], 1, opens=True, closes=False)
-        look_up(last, banks[last], 0, opens=False, closes=True)
+        for piece in range(EARLY, len(PIECES)):
+            look_up(piece, banks[piece], 1, opens=True, closes=False)
+            look_up(piece, banks[piece], 0, opens=False, closes=True)
         for piece in range(len(PIECES)):
             finish(piece, banks[piece])
         nc.sync.dma_start(out, means[:])

@@ -8,6 +8,8 @@ S = 1024
 K_BLOCKS = 2
 N = 768
 GROUP = 8
+BANK = 512
+WARM_UPS = 3
 PIECES = (256, 256, 128, 128)
 EARLY = 2
 STARTS = tuple(sum(PIECES[:piece]) for piece in range(len(PIECES)))
@@ -59,6 +61,12 @@ def tile_gather_matmul_kernel(tc, table, w, b, offs, out):
             nc.vector.reduce_sum(pooled[:], z[:].rearrange("p (v t) -> p v t", t=GROUP), axis=mybir.AxisListType.X)
             first = STARTS[piece] // GROUP
             nc.vector.tensor_scalar_mul(means[:, first : first + PIECES[piece] // GROUP], pooled[:], 1.0 / GROUP)
+
+        still = held.tile([P, BANK], BF16, name="still")
+        nc.vector.memset(still[:], 0.0)
+        unread = psum.tile([P, BANK], F32, name="unread")
+        for turn in range(WARM_UPS):
+            nc.tensor.matmul(unread[:], still[:, 0:P], still[:], start=True, stop=True)
 
         banks = [psum.tile([P, PIECES[piece]], F32, name="bank%d" % piece) for piece in range(len(PIECES))]
         for a in range(K_BLOCKS):

@@ -31,10 +31,10 @@ def tile_gather_matmul_kernel(tc, table, w, b, offs, out):
         for a in range(K_BLOCKS):
             nc.sync.dma_start(blocks[a][:], table[a * P : (a + 1) * P, :])
 
-        weights = held.tile([P, K_BLOCKS, P], BF16, name="weights")
-        nc.scalar.dma_start(weights[:], w.rearrange("(a p) m -> p a m", p=P))
         bias = held.tile([P, 1], F32, name="bias")
         nc.scalar.dma_start(bias[:], b)
+        weights = held.tile([P, K_BLOCKS, P], BF16, name="weights")
+        nc.scalar.dma_start(weights[:], w.rearrange("(a p) m -> p a m", p=P))
 
         zeros = held.tile([P, 1], F32, name="zeros")
         nc.gpsimd.memset(zeros[:], 0.0)

@@ -25,16 +25,18 @@ def tile_gather_matmul_kernel(tc, table, w, b, offs, out):
         tc.tile_pool(name="work", bufs=len(PIECES)) as work,
         tc.psum_pool(name="psum", bufs=1) as psum,
     ):
+        by_block = table.rearrange("(p a) s -> p a s", a=K_BLOCKS)
+
         offsets = held.tile([P, N // 16], U16, name="offsets")
         nc.sync.dma_start(offsets[:], offs)
         blocks = [held.tile([P, S], BF16, name="block%d" % a) for a in range(K_BLOCKS)]
         for a in range(K_BLOCKS):
-            nc.sync.dma_start(blocks[a][:], table[a * P : (a + 1) * P, :])
+            nc.sync.dma_start(blocks[a][:], by_block[:, a, :])
 
         bias = held.tile([P, 1], F32, name="bias")
         nc.scalar.dma_start(bias[:], b)
         weights = held.tile([P, K_BLOCKS, P], BF16, name="weights")
-        nc.scalar.dma_start(weights[:], w.rearrange("(a p) m -> p a m", p=P))
+        nc.scalar.dma_start(weights[:], w.rearrange("(p a) m -> p a m", a=K_BLOCKS))
 
         zeros = held.tile([P, 1], F32, name="zeros")
         nc.gpsimd.memset(zeros[:], 0.0)

@@ -8,8 +8,6 @@ S = 1024
 K_BLOCKS = 2
 N = 768
 GROUP = 8
-BANK = 512
-WARM_UPS = 3
 PIECES = (256, 256, 128, 128)
 EARLY = 2
 STARTS = tuple(sum(PIECES[:piece]) for piece in range(len(PIECES)))
@@ -63,12 +61,6 @@ def tile_gather_matmul_kernel(tc, table, w, b, offs, out):
             nc.vector.reduce_sum(pooled[:], z[:].rearrange("p (v t) -> p v t", t=GROUP), axis=mybir.AxisListType.X)
             first = STARTS[piece] // GROUP
             nc.vector.tensor_scalar_mul(means[:, first : first + PIECES[piece] // GROUP], pooled[:], 1.0 / GROUP)
-
-        still = held.tile([P, BANK], BF16, name="still")
-        nc.vector.memset(still[:], 0.0)
-        unread = psum.tile([P, BANK], F32, name="unread")
-        for turn in range(WARM_UPS):
-            nc.tensor.matmul(unread[:], still[:, 0:P], still[:], start=True, stop=True)
 
         banks = [psum.tile([P, PIECES[piece]], F32, name="bank%d" % piece) for piece in range(len(PIECES))]
         for a in range(K_BLOCKS):

import concourse.mybir as mybir

BF16, F32, U16 = mybir.dt.bfloat16, mybir.dt.float32, mybir.dt.uint16
GELU_TANH = mybir.ActivationFunctionType.Gelu_apprx_tanh

P = 128
S = 1024
K_BLOCKS = 2
N = 768
GROUP = 8
PIECES = (256, 256, 128, 128)
EARLY = 2
STARTS = tuple(sum(PIECES[:piece]) for piece in range(len(PIECES)))
assert sum(PIECES) == N

FLOPS = 2 * K_BLOCKS * P * P * N


def tile_gather_matmul_kernel(tc, table, w, b, offs, out):
    nc = tc.nc
    with (
        tc.tile_pool(name="held", bufs=1) as held,
        tc.tile_pool(name="work", bufs=len(PIECES)) as work,
        tc.psum_pool(name="psum", bufs=1) as psum,
    ):
        by_block = table.rearrange("(p a) s -> p a s", a=K_BLOCKS)

        offsets = held.tile([P, N // 16], U16, name="offsets")
        nc.sync.dma_start(offsets[:], offs)
        blocks = [held.tile([P, S], BF16, name="block%d" % a) for a in range(K_BLOCKS)]
        for a in range(K_BLOCKS):
            nc.sync.dma_start(blocks[a][:], by_block[:, a, :])

        bias = held.tile([P, 1], F32, name="bias")
        nc.scalar.dma_start(bias[:], b)
        weights = held.tile([P, K_BLOCKS, P], BF16, name="weights")
        nc.scalar.dma_start(weights[:], w.rearrange("(p a) m -> p a m", a=K_BLOCKS))

        zeros = held.tile([P, 1], F32, name="zeros")
        nc.gpsimd.memset(zeros[:], 0.0)
        warmed = held.tile([P, 1], F32, name="warmed")
        nc.scalar.activation(warmed[:], zeros[:], GELU_TANH)

        means = held.tile([P, N // GROUP], F32, name="means")

        def look_up(piece, bank, a, opens, closes):
            first = STARTS[piece] // 16
            picked = offsets[:, first : first + PIECES[piece] // 16]
            nc.tensor.matmul(
                bank[:],
                weights[:, a, :],
                blocks[a][:].indirect(picked),
                start=opens,
                stop=closes,
            )

        def finish(piece, bank):
            z = work.tile([P, PIECES[piece]], F32, name="z")
            nc.scalar.activation(z[:], bank[:], GELU_TANH, bias=bias[:, 0:1])
            pooled = work.tile([P, PIECES[piece] // GROUP], F32, name="pooled")
            nc.vector.reduce_sum(pooled[:], z[:].rearrange("p (v t) -> p v t", t=GROUP), axis=mybir.AxisListType.X)
            first = STARTS[piece] // GROUP
            nc.vector.tensor_scalar_mul(means[:, first : first + PIECES[piece] // GROUP], pooled[:], 1.0 / GROUP)

        banks = [psum.tile([P, PIECES[piece]], F32, name="bank%d" % piece) for piece in range(len(PIECES))]
        for a in range(K_BLOCKS):
            for piece in range(EARLY):
                look_up(piece, banks[piece], a, opens=(a == 0), closes=(a == K_BLOCKS - 1))
        for piece in range(EARLY, len(PIECES)):
            look_up(piece, banks[piece], 1, opens=True, closes=False)
            look_up(piece, banks[piece], 0, opens=False, closes=True)
        for piece in range(len(PIECES)):
            finish(piece, banks[piece])
        nc.sync.dma_start(out, means[:])
